import numpy as np
import ml_dtypes


def mxq(x, axis, fmt="e4m3"):
    dtype, down = {"e4m3": (ml_dtypes.float8_e4m3fn, 7), "e5m2": (ml_dtypes.float8_e5m2, 14)}[fmt]
    v = np.moveaxis(np.asarray(x, np.float32).astype(ml_dtypes.bfloat16).astype(np.float64), axis, -1)
    blocks = v.reshape(v.shape[:-1] + (-1, 32))
    amax = np.abs(blocks).max(-1, keepdims=True)
    byte = np.maximum(np.where(amax > 0, np.frexp(amax)[1] - 1 + 127, 0) - down, 1)
    scale = np.exp2(byte - 127.0)
    codes = (blocks / scale).astype(np.float32).astype(dtype).astype(np.float64)
    return np.moveaxis((codes * scale).reshape(v.shape), -1, axis)


WIDE = False


def mx_kscale(k):
    if not WIDE:
        return np.ones(k)
    levels = np.array([18, -18])
    if k % 512:
        return np.exp2(np.random.permutation(np.resize(levels, k // 32))).repeat(32)
    a = np.empty((k // 512, 16))
    for p in range(k // 512):
        a[p, :8] = np.random.permutation(np.resize(levels, 8))
        for g in range(8):
            far = levels[np.abs(levels - a[p, g]) >= 10]
            a[p, g + 8] = far[np.random.randint(len(far))]
    return np.exp2(a.ravel()).repeat(32)


def f64(x):
    return np.asarray(x).astype(np.float64)


def striped(idx):
    return np.tile(np.asarray(idx).reshape(-1, 16).T, (8, 1)).astype(np.uint16)


def unstriped(offs):
    return offs[:16].T.reshape(-1).astype(np.int64)


B, N, T, D, R = 1, 512, 2048, 512, 1024


def setup_inputs():
    n = np.random.standard_normal
    idx = np.random.permutation(T)[:B * N]
    u = np.ones(T)
    u[idx] = mx_kscale(B * N)
    us = u[idx].reshape(B, N)
    act = n((B, R, N))
    s = mx_kscale(D)
    return {
        "zT": (act.transpose(0, 2, 1) * us[:, :, None]).astype(np.float32),
        "wT": (n((D, T)) / np.sqrt(N) / u * s[:, None]).astype(np.float32),
        "xm": (n((B, R, D)) * s).astype(np.float32),
        "wt": (np.random.uniform(0.5, 1.5, (B, R, 1)) / np.sqrt(R)).astype(np.float32),
        "cs": np.tile(np.random.uniform(0.5, 1.5, D) / s, (128, 1)).astype(np.float32),
        "offs": striped(idx),
    }


def reference(zT, wT, xm, wt, cs, offs):
    idx = unstriped(offs)
    pick = lambda x: x[:, idx].reshape(x.shape[0], B, N).transpose(1, 0, 2)
    w = pick(f64(wT))
    rec = mxq(f64(zT), 1, "e4m3").transpose(0, 2, 1) @ mxq(w, 2, "e4m3").transpose(0, 2, 1)
    q = f64(cs)[:1] * (rec - f64(xm))
    e = f64(wt) * f64(cs)[:1] * np.minimum(np.maximum(q, -1.0), 1.0)
    gz = mxq(e, 2, "e5m2") @ mxq(w, 1, "e4m3")
    return gz

@@ -1,0 +1,226 @@
+from contextlib import ExitStack
+
+import concourse.mybir as mybir
+from concourse.masks import make_identity
+
+N, T, D, R = 512, 2048, 512, 1024
+FLOPS = 2 * 2 * R * N * D
+
+F32 = mybir.dt.float32
+BF16 = mybir.dt.bfloat16
+U32 = mybir.dt.uint32
+U16 = mybir.dt.uint16
+U8 = mybir.dt.uint8
+E4M3 = mybir.dt.float8_e4m3fn_x4
+E5M2 = mybir.dt.float8_e5m2_x4
+ALU = mybir.AluOpType
+COPY = mybir.ActivationFunctionType.Copy
+
+P = 128
+PACK = 4
+TILES = R // P
+QR = 256
+QUARTERS = R // QR
+
+
+def tile_attend_gdi_hub_z_kernel(tc, zT, wT, xm, wt, cs, offs, out):
+    nc = tc.nc
+    with ExitStack() as ctx:
+        keep = ctx.enter_context(tc.tile_pool(name="keep", bufs=1))
+        psum = ctx.enter_context(tc.psum_pool(name="psum", bufs=1))
+
+        offsets = keep.tile([P, N // 16], U16, name="offsets")
+        nc.sync.dma_start(offsets[:], offs)
+        wt_cols = keep.tile([P, 2, PACK], F32, name="wt_cols")
+        nc.scalar.dma_start(out=wt_cols[:], in_=wt[0].rearrange("(h p j) o -> p h (j o)", h=2, j=PACK))
+        cs_cols = keep.tile([P, PACK], F32, name="cs_cols")
+        nc.scalar.dma_start(out=cs_cols[:], in_=cs[0:1, :].rearrange("o (p t) -> p (o t)", t=PACK))
+        w_rows = wT.rearrange("(p t) n -> t p n", t=PACK)
+        planes = []
+        for t in range(PACK):
+            plane = keep.tile([P, T], F32, name="plane%d" % t)
+            nc.sync.dma_start(out=plane[:], in_=w_rows[t])
+            planes.append(plane)
+        z_rows = zT[0].rearrange("(p j) r -> p j r", j=PACK)
+        z_pieces = [(0, 1), (1, 1), (2, 2), (4, 2), (6, 2)]
+        z_raw, x_raw = {}, []
+        for first, count in z_pieces:
+            piece = keep.tile([P, PACK, count * P], F32, name="z_raw%d" % first, tag="z_raw%d" % first, align_bytes=64)
+            nc.sync.dma_start(out=piece[:], in_=z_rows[:, :, first * P : (first + count) * P])
+            z_raw[first] = piece
+            if (first + count) % 2 == 0:
+                q = first // 2
+                xq = keep.tile([P, 2, D], F32, name="x_raw%d" % q, tag="x_raw%d" % q, align_bytes=64)
+                nc.sync.dma_start(out=xq[:], in_=xm[0, q * QR : (q + 1) * QR, :].rearrange("(a m) d -> m a d", a=2))
+                x_raw.append(xq)
+
+        ident = keep.tile([P, P], F32, name="ident")
+        make_identity(nc, ident[:])
+
+        factor = keep.tile([P, PACK * R], F32, name="factor")
+        for h in range(2):
+            bank = psum.tile([P, PACK, P], F32, name="wt_bank%d" % h, tag="out", bufs=2)
+            for j in range(PACK):
+                nc.tensor.transpose(bank[:, j, :], wt_cols[:, h, j : j + 1].to_broadcast([P, P]), ident[:])
+            for t in range(PACK):
+                nc.scalar.activation(
+                    out=factor[:, t * R + h * 512 : t * R + (h + 1) * 512].rearrange("p (m j) -> p m j", j=PACK),
+                    in_=bank[:].rearrange("p j m -> p m j"),
+                    func=COPY,
+                    scale=cs_cols[:, t : t + 1],
+                )
+
+        atoms = keep.tile([P, PACK * N], BF16, name="atoms", align_bytes=64)
+        w1_bf = keep.tile([P, D * PACK], BF16, name="w1_bf", align_bytes=64)
+        w1_codes = keep.tile([P, D], U32, name="w1_codes", align_bytes=64)
+        w1_scales = keep.tile([P, D], U8, name="w1_scales", align_bytes=64)
+        for t in range(PACK):
+            nc.vector.tensor_copy(out=atoms[:, t * N : (t + 1) * N], in_=planes[t][:].indirect(offsets[:]))
+            words = atoms[:, t * N : (t + 1) * N].bitcast(F32)
+            bank = psum.tile([P, 2, P], F32, name="w_bank%d" % t, tag="turn", bufs=4)
+            for u in range(2):
+                nc.tensor.transpose(bank[:, u, :], words[:, u : N // 2 : 2], ident[:])
+            dst = w1_bf[:, t * P * PACK : (t + 1) * P * PACK]
+            copy_out = nc.vector.tensor_copy if t == PACK - 1 else nc.scalar.copy
+            copy_out(out=dst.bitcast(F32).rearrange("p (c u) -> p c u", u=2), in_=bank[:].rearrange("p u c -> p c u"))
+            nc.vector.quantize_mx(
+                out=w1_codes[:, t * P : (t + 1) * P].bitcast(E4M3), scales=w1_scales[:, t * P : (t + 1) * P], in_=dst
+            )
+
+        z_codes, z_scales = {}, {}
+        diff = [keep.tile([P, D], F32, name="diff%d" % j) for j in range(TILES)]
+        scaled, clipped, w2 = {}, {}, {}
+        e_bf = [keep.tile([P, P * PACK], BF16, name="e_bf%d" % j, align_bytes=64) for j in range(TILES)]
+
+        def prepare_z(piece):
+            first, count = z_pieces[piece]
+            z_bf = keep.tile([P, count * P * PACK], BF16, name="z_bf%d" % first, tag="z_bf%d" % first, align_bytes=64)
+            nc.scalar.copy(
+                out=z_bf[:].rearrange("p (c i t) -> p c t i", i=2, t=PACK),
+                in_=z_raw[first][:].rearrange("p t (c i) -> p c t i", i=2),
+            )
+            codes = keep.tile([P, count * P], U32, name="z_codes%d" % first, align_bytes=64)
+            scales = keep.tile([P, count * P], U8, name="z_scales%d" % first, align_bytes=64)
+            nc.vector.quantize_mx(out=codes[:].bitcast(E4M3), scales=scales[:], in_=z_bf[:])
+            for a in range(count):
+                z_codes[first + a] = codes[:, a * P : (a + 1) * P]
+                z_scales[first + a] = scales[:, a * P : (a + 1) * P]
+
+        def weave_atoms(half, tag):
+            woven = keep.tile([P, 256 * PACK], BF16, name="w2_bf%d" % half, tag=tag, align_bytes=64)
+            src = atoms[:].rearrange("p (t s) -> p t s", t=PACK)[:, :, half * 256 : (half + 1) * 256]
+            nc.vector.tensor_copy(
+                out=woven[:].rearrange("p (c i t) -> p c t i", i=4, t=PACK),
+                in_=src.rearrange("p t (c i) -> p c t i", i=4),
+            )
+            return woven
+
+        def residual(j):
+            q, a = divmod(j, 2)
+            rec = psum.tile([P, D], F32, name="rec%d" % j, tag="rec", bufs=2)
+            nc.tensor.matmul_mx(
+                out=rec[:],
+                lhsT=z_codes[j].bitcast(E4M3),
+                lhsT_scale=z_scales[j],
+                rhs=w1_codes[:].bitcast(E4M3),
+                rhs_scale=w1_scales[:],
+                start=True,
+                stop=True,
+            )
+            nc.vector.tensor_tensor(
+                out=diff[j][:].rearrange("m (u p e) -> m u p e", u=2, e=2),
+                in0=rec[:].rearrange("m (u e p) -> m u p e", u=2, e=2),
+                in1=x_raw[q][:, a, :].rearrange("m (p u e) -> m u p e", u=2, e=2),
+                op=ALU.subtract,
+            )
+
+        def turn(q):
+            tag = "z_raw%d" % (2 * q + 4) if q + 2 < QUARTERS else "scaled%d" % q
+            scaled[q] = keep.tile([P, PACK * QR], F32, name="scaled%d" % q, tag=tag, align_bytes=64)
+            for u in range(2):
+                bank = psum.tile([P, 2, QR], F32, name="d_bank%d_%d" % (q, u), tag="turn", bufs=4)
+                for a in range(2):
+                    for e in range(2):
+                        nc.tensor.transpose(
+                            bank[:, e, a * P : (a + 1) * P],
+                            diff[2 * q + a][:, u * 256 + e : (u + 1) * 256 : 2],
+                            ident[:],
+                        )
+                for e in range(2):
+                    t = 2 * u + e
+                    nc.scalar.activation(
+                        out=scaled[q][:, t * QR : (t + 1) * QR], in_=bank[:, e, :], func=COPY, scale=cs_cols[:, t : t + 1]
+                    )
+
+        def clip(q):
+            tag = "x_raw%d" % (q + 2) if q + 2 < QUARTERS else "clipped%d" % q
+            clipped[q] = keep.tile([P, PACK * QR], F32, name="clipped%d" % q, tag=tag, align_bytes=64)
+            nc.vector.tensor_scalar(
+                out=clipped[q][:], in0=scaled[q][:], scalar1=-1.0, scalar2=1.0, op0=ALU.max, op1=ALU.min
+            )
+
+        def weigh(j):
+            q, a = divmod(j, 2)
+            c_view = clipped[q][:].rearrange("p (t r) -> p t r", t=PACK)[:, :, a * P : (a + 1) * P]
+            f_view = factor[:].rearrange("p (t r) -> p t r", t=PACK)[:, :, j * P : (j + 1) * P]
+            nc.vector.tensor_tensor(
+                out=e_bf[j][:].rearrange("p (c i t) -> p c t i", i=2, t=PACK),
+                in0=c_view.rearrange("p t (c i) -> p c t i", i=2),
+                in1=f_view.rearrange("p t (c i) -> p c t i", i=2),
+                op=ALU.mult,
+            )
+
+        def gradient(j):
+            e_codes = keep.tile([P, P], U32, name="e_codes%d" % j, align_bytes=64)
+            e_scales = keep.tile([P, P], U8, name="e_scales%d" % j, align_bytes=64)
+            nc.vector.quantize_mx(out=e_codes[:].bitcast(E5M2), scales=e_scales[:], in_=e_bf[j][:])
+            acc = psum.tile([P, N], F32, name="acc%d" % j, tag="rec" if (j // 2) % 2 else "out", bufs=2)
+            nc.tensor.matmul_mx(
+                out=acc[:],
+                lhsT=e_codes[:].bitcast(E5M2),
+                lhsT_scale=e_scales[:],
+                rhs=w2["codes"][:].bitcast(E4M3),
+                rhs_scale=w2["scales"][:],
+                start=True,
+                stop=True,
+            )
+            result = keep.tile([P, N], F32, name="result%d" % j)
+            copy_out = nc.vector.tensor_copy if j == TILES - 1 else nc.scalar.copy
+            copy_out(out=result[:], in_=acc[:])
+            nc.sync.dma_start(out=out[0, j * P : (j + 1) * P, :], in_=result[:])
+
+        def finish(q):
+            clip(q)
+            weigh(2 * q)
+            weigh(2 * q + 1)
+            gradient(2 * q)
+            gradient(2 * q + 1)
+
+        prepare_z(0)
+        prepare_z(1)
+        woven = [weave_atoms(0, "w2_bf0")]
+        residual(0)
+        residual(1)
+        woven.append(weave_atoms(1, "z_bf1"))
+        w2["codes"] = keep.tile([P, N], U32, name="w2_codes", tag="z_raw1", align_bytes=64)
+        w2["scales"] = keep.tile([P, N], U8, name="w2_scales", align_bytes=64)
+        prepare_z(2)
+        residual(2)
+        residual(3)
+        for half in range(2):
+            cols = slice(half * 256, (half + 1) * 256)
+            nc.vector.quantize_mx(out=w2["codes"][:, cols].bitcast(E4M3), scales=w2["scales"][:, cols], in_=woven[half][:])
+        prepare_z(3)
+        turn(0)
+        residual(4)
+        residual(5)
+        prepare_z(4)
+        turn(1)
+        finish(0)
+        residual(6)
+        residual(7)
+        turn(2)
+        turn(3)
+        finish(1)
+        finish(2)
+        finish(3)

@@ -42,24 +42,36 @@ def tile_attend_gdi_hub_z_kernel(tc, zT, wT, xm, wt, cs, offs, out):
             nc.sync.dma_start(out=plane[:], in_=w_rows[t])
             planes.append(plane)
         z_rows = zT[0].rearrange("(p j) r -> p j r", j=PACK)
-        z_pieces = [(0, 1), (1, 1), (2, 2), (4, 2), (6, 2)]
-        z_raw, x_raw = {}, []
-        for first, count in z_pieces:
+        z_raw, x_raw = {}, {}
+
+        def load_z(first, count):
             piece = keep.tile([P, PACK, count * P], F32, name="z_raw%d" % first, tag="z_raw%d" % first, align_bytes=64)
             nc.sync.dma_start(out=piece[:], in_=z_rows[:, :, first * P : (first + count) * P])
-            z_raw[first] = piece
-            if (first + count) % 2 == 0:
-                q = first // 2
-                xq = keep.tile([P, 2, D], F32, name="x_raw%d" % q, tag="x_raw%d" % q, align_bytes=64)
-                nc.sync.dma_start(out=xq[:], in_=xm[0, q * QR : (q + 1) * QR, :].rearrange("(a m) d -> m a d", a=2))
-                x_raw.append(xq)
+            for a in range(count):
+                z_raw[first + a] = piece[:, :, a * P : (a + 1) * P]
+
+        def load_x(first):
+            piece = keep.tile([P, 2, D], F32, name="x_raw%d" % first)
+            nc.sync.dma_start(
+                out=piece[:], in_=xm[0, first * P : (first + 2) * P, :].rearrange("(a m) d -> m a d", a=2)
+            )
+            for a in range(2):
+                x_raw[first + a] = piece[:, a, :]
+
+        load_z(0, 2)
+        load_x(0)
+        load_z(2, 2)
+        load_x(2)
+        load_z(4, 4)
+        load_x(4)
+        load_x(6)
 
         ident = keep.tile([P, P], F32, name="ident")
         make_identity(nc, ident[:])
 
         factor = keep.tile([P, PACK * R], F32, name="factor")
         for h in range(2):
-            bank = psum.tile([P, PACK, P], F32, name="wt_bank%d" % h, tag="out", bufs=2)
+            bank = psum.tile([P, PACK, P], F32, name="wt_bank%d" % h, tag="out", bufs=3)
             for j in range(PACK):
                 nc.tensor.transpose(bank[:, j, :], wt_cols[:, h, j : j + 1].to_broadcast([P, P]), ident[:])
             for t in range(PACK):
@@ -77,7 +89,7 @@ def tile_attend_gdi_hub_z_kernel(tc, zT, wT, xm, wt, cs, offs, out):
         for t in range(PACK):
             nc.vector.tensor_copy(out=atoms[:, t * N : (t + 1) * N], in_=planes[t][:].indirect(offsets[:]))
             words = atoms[:, t * N : (t + 1) * N].bitcast(F32)
-            bank = psum.tile([P, 2, P], F32, name="w_bank%d" % t, tag="turn", bufs=4)
+            bank = psum.tile([P, 2, P], F32, name="w_bank%d" % t, tag="turn", bufs=3)
             for u in range(2):
                 nc.tensor.transpose(bank[:, u, :], words[:, u : N // 2 : 2], ident[:])
             dst = w1_bf[:, t * P * PACK : (t + 1) * P * PACK]
@@ -89,22 +101,18 @@ def tile_attend_gdi_hub_z_kernel(tc, zT, wT, xm, wt, cs, offs, out):
 
         z_codes, z_scales = {}, {}
         diff = [keep.tile([P, D], F32, name="diff%d" % j) for j in range(TILES)]
-        scaled, clipped, w2 = {}, {}, {}
+        scaled, clipped, w2, accs = {}, {}, {}, {}
         e_bf = [keep.tile([P, P * PACK], BF16, name="e_bf%d" % j, align_bytes=64) for j in range(TILES)]
 
-        def prepare_z(piece):
-            first, count = z_pieces[piece]
-            z_bf = keep.tile([P, count * P * PACK], BF16, name="z_bf%d" % first, tag="z_bf%d" % first, align_bytes=64)
+        def prepare_z(j):
+            z_bf = keep.tile([P, P * PACK], BF16, name="z_bf%d" % j, tag="z_bf%d" % j, align_bytes=64)
             nc.scalar.copy(
                 out=z_bf[:].rearrange("p (c i t) -> p c t i", i=2, t=PACK),
-                in_=z_raw[first][:].rearrange("p t (c i) -> p c t i", i=2),
+                in_=z_raw[j].rearrange("p t (c i) -> p c t i", i=2),
             )
-            codes = keep.tile([P, count * P], U32, name="z_codes%d" % first, align_bytes=64)
-            scales = keep.tile([P, count * P], U8, name="z_scales%d" % first, align_bytes=64)
-            nc.vector.quantize_mx(out=codes[:].bitcast(E4M3), scales=scales[:], in_=z_bf[:])
-            for a in range(count):
-                z_codes[first + a] = codes[:, a * P : (a + 1) * P]
-                z_scales[first + a] = scales[:, a * P : (a + 1) * P]
+            z_codes[j] = keep.tile([P, P], U32, name="z_codes%d" % j, align_bytes=64)
+            z_scales[j] = keep.tile([P, P], U8, name="z_scales%d" % j, align_bytes=64)
+            nc.vector.quantize_mx(out=z_codes[j][:].bitcast(E4M3), scales=z_scales[j][:], in_=z_bf[:])
 
         def weave_atoms(half, tag):
             woven = keep.tile([P, 256 * PACK], BF16, name="w2_bf%d" % half, tag=tag, align_bytes=64)
@@ -116,12 +124,11 @@ def tile_attend_gdi_hub_z_kernel(tc, zT, wT, xm, wt, cs, offs, out):
             return woven
 
         def residual(j):
-            q, a = divmod(j, 2)
             rec = psum.tile([P, D], F32, name="rec%d" % j, tag="rec", bufs=2)
             nc.tensor.matmul_mx(
                 out=rec[:],
-                lhsT=z_codes[j].bitcast(E4M3),
-                lhsT_scale=z_scales[j],
+                lhsT=z_codes[j][:].bitcast(E4M3),
+                lhsT_scale=z_scales[j][:],
                 rhs=w1_codes[:].bitcast(E4M3),
                 rhs_scale=w1_scales[:],
                 start=True,
@@ -130,42 +137,32 @@ def tile_attend_gdi_hub_z_kernel(tc, zT, wT, xm, wt, cs, offs, out):
             nc.vector.tensor_tensor(
                 out=diff[j][:].rearrange("m (u p e) -> m u p e", u=2, e=2),
                 in0=rec[:].rearrange("m (u e p) -> m u p e", u=2, e=2),
-                in1=x_raw[q][:, a, :].rearrange("m (p u e) -> m u p e", u=2, e=2),
+                in1=x_raw[j].rearrange("m (p u e) -> m u p e", u=2, e=2),
                 op=ALU.subtract,
             )
 
-        def turn(q):
-            tag = "z_raw%d" % (2 * q + 4) if q + 2 < QUARTERS else "scaled%d" % q
-            scaled[q] = keep.tile([P, PACK * QR], F32, name="scaled%d" % q, tag=tag, align_bytes=64)
-            for u in range(2):
-                bank = psum.tile([P, 2, QR], F32, name="d_bank%d_%d" % (q, u), tag="turn", bufs=4)
-                for a in range(2):
-                    for e in range(2):
-                        nc.tensor.transpose(
-                            bank[:, e, a * P : (a + 1) * P],
-                            diff[2 * q + a][:, u * 256 + e : (u + 1) * 256 : 2],
-                            ident[:],
-                        )
-                for e in range(2):
-                    t = 2 * u + e
-                    nc.scalar.activation(
-                        out=scaled[q][:, t * QR : (t + 1) * QR], in_=bank[:, e, :], func=COPY, scale=cs_cols[:, t : t + 1]
-                    )
+        def turn(j):
+            scaled[j] = keep.tile([P, PACK * P], F32, name="scaled%d" % j)
+            bank = psum.tile([P, PACK, P], F32, name="d_bank%d" % j, tag="turn", bufs=3)
+            for t in range(PACK):
+                u, e = divmod(t, 2)
+                nc.tensor.transpose(bank[:, t, :], diff[j][:, u * 256 + e : (u + 1) * 256 : 2], ident[:])
+            for t in range(PACK):
+                nc.scalar.activation(
+                    out=scaled[j][:, t * P : (t + 1) * P], in_=bank[:, t, :], func=COPY, scale=cs_cols[:, t : t + 1]
+                )
 
-        def clip(q):
-            tag = "x_raw%d" % (q + 2) if q + 2 < QUARTERS else "clipped%d" % q
-            clipped[q] = keep.tile([P, PACK * QR], F32, name="clipped%d" % q, tag=tag, align_bytes=64)
+        def clip(j):
+            clipped[j] = keep.tile([P, PACK * P], F32, name="clipped%d" % j)
             nc.vector.tensor_scalar(
-                out=clipped[q][:], in0=scaled[q][:], scalar1=-1.0, scalar2=1.0, op0=ALU.max, op1=ALU.min
+                out=clipped[j][:], in0=scaled[j][:], scalar1=-1.0, scalar2=1.0, op0=ALU.max, op1=ALU.min
             )
 
         def weigh(j):
-            q, a = divmod(j, 2)
-            c_view = clipped[q][:].rearrange("p (t r) -> p t r", t=PACK)[:, :, a * P : (a + 1) * P]
             f_view = factor[:].rearrange("p (t r) -> p t r", t=PACK)[:, :, j * P : (j + 1) * P]
             nc.vector.tensor_tensor(
                 out=e_bf[j][:].rearrange("p (c i t) -> p c t i", i=2, t=PACK),
-                in0=c_view.rearrange("p t (c i) -> p c t i", i=2),
+                in0=clipped[j][:].rearrange("p (t c i) -> p c t i", t=PACK, i=2),
                 in1=f_view.rearrange("p t (c i) -> p c t i", i=2),
                 op=ALU.mult,
             )
@@ -174,7 +171,7 @@ def tile_attend_gdi_hub_z_kernel(tc, zT, wT, xm, wt, cs, offs, out):
             e_codes = keep.tile([P, P], U32, name="e_codes%d" % j, align_bytes=64)
             e_scales = keep.tile([P, P], U8, name="e_scales%d" % j, align_bytes=64)
             nc.vector.quantize_mx(out=e_codes[:].bitcast(E5M2), scales=e_scales[:], in_=e_bf[j][:])
-            acc = psum.tile([P, N], F32, name="acc%d" % j, tag="rec" if (j // 2) % 2 else "out", bufs=2)
+            acc = psum.tile([P, N], F32, name="acc%d" % j, tag="out", bufs=3)
             nc.tensor.matmul_mx(
                 out=acc[:],
                 lhsT=e_codes[:].bitcast(E5M2),
@@ -184,43 +181,49 @@ def tile_attend_gdi_hub_z_kernel(tc, zT, wT, xm, wt, cs, offs, out):
                 start=True,
                 stop=True,
             )
-            result = keep.tile([P, N], F32, name="result%d" % j)
-            copy_out = nc.vector.tensor_copy if j == TILES - 1 else nc.scalar.copy
-            copy_out(out=result[:], in_=acc[:])
-            nc.sync.dma_start(out=out[0, j * P : (j + 1) * P, :], in_=result[:])
+            accs[j] = acc
 
-        def finish(q):
-            clip(q)
-            weigh(2 * q)
-            weigh(2 * q + 1)
-            gradient(2 * q)
-            gradient(2 * q + 1)
+        def store(j):
+            acc = accs[j]
+            result = keep.tile([P, N], F32, name="result%d" % j)
+            rows = out[0, j * P : (j + 1) * P, :]
+            if j < TILES - 1:
+                nc.scalar.copy(out=result[:], in_=acc[:])
+                nc.sync.dma_start(out=rows, in_=result[:])
+            else:
+                for half in range(2):
+                    cols = slice(half * 256, (half + 1) * 256)
+                    nc.vector.tensor_copy(out=result[:, cols], in_=acc[:, cols])
+                    nc.sync.dma_start(out=rows[:, cols], in_=result[:, cols])
 
         prepare_z(0)
         prepare_z(1)
         woven = [weave_atoms(0, "w2_bf0")]
         residual(0)
+        turn(0)
         residual(1)
+        turn(1)
         woven.append(weave_atoms(1, "z_bf1"))
-        w2["codes"] = keep.tile([P, N], U32, name="w2_codes", tag="z_raw1", align_bytes=64)
+        w2["codes"] = keep.tile([P, N], U32, name="w2_codes", tag="z_raw0", align_bytes=64)
         w2["scales"] = keep.tile([P, N], U8, name="w2_scales", align_bytes=64)
         prepare_z(2)
         residual(2)
-        residual(3)
+        turn(2)
+        prepare_z(3)
         for half in range(2):
             cols = slice(half * 256, (half + 1) * 256)
             nc.vector.quantize_mx(out=w2["codes"][:, cols].bitcast(E4M3), scales=w2["scales"][:, cols], in_=woven[half][:])
-        prepare_z(3)
-        turn(0)
-        residual(4)
-        residual(5)
-        prepare_z(4)
-        turn(1)
-        finish(0)
-        residual(6)
-        residual(7)
-        turn(2)
-        turn(3)
-        finish(1)
-        finish(2)
-        finish(3)
+        clip(0)
+        for s in range(TILES):
+            if s + 3 < TILES:
+                residual(s + 3)
+                turn(s + 3)
+            if s + 4 < TILES:
+                prepare_z(s + 4)
+            weigh(s)
+            if s + 1 < TILES:
+                clip(s + 1)
+            gradient(s)
+            if s >= 1:
+                store(s - 1)
+        store(TILES - 1)

@@ -38,7 +38,7 @@ def tile_attend_gdi_hub_z_kernel(tc, zT, wT, xm, wt, cs, offs, out):
         w_rows = wT.rearrange("(p t) n -> t p n", t=PACK)
         planes = []
         for t in range(PACK):
-            plane = keep.tile([P, T], F32, name="plane%d" % t)
+            plane = keep.tile([P, T], F32, name="plane%d" % t, tag="plane%d" % t, align_bytes=64)
             nc.sync.dma_start(out=plane[:], in_=w_rows[t])
             planes.append(plane)
         z_rows = zT[0].rearrange("(p j) r -> p j r", j=PACK)
@@ -58,20 +58,18 @@ def tile_attend_gdi_hub_z_kernel(tc, zT, wT, xm, wt, cs, offs, out):
             for a in range(2):
                 x_raw[first + a] = piece[:, a, :]
 
-        load_z(0, 2)
-        load_x(0)
-        load_z(2, 2)
-        load_x(2)
-        load_z(4, 4)
-        load_x(4)
-        load_x(6)
+        for half in range(2):
+            load_z(4 * half, 2)
+            load_z(4 * half + 2, 2)
+            load_x(4 * half)
+            load_x(4 * half + 2)
 
         ident = keep.tile([P, P], F32, name="ident")
         make_identity(nc, ident[:])
 
         factor = keep.tile([P, PACK * R], F32, name="factor")
         for h in range(2):
-            bank = psum.tile([P, PACK, P], F32, name="wt_bank%d" % h, tag="out", bufs=3)
+            bank = psum.tile([P, PACK, P], F32, name="wt_bank%d" % h, tag="out", bufs=2)
             for j in range(PACK):
                 nc.tensor.transpose(bank[:, j, :], wt_cols[:, h, j : j + 1].to_broadcast([P, P]), ident[:])
             for t in range(PACK):
@@ -83,21 +81,33 @@ def tile_attend_gdi_hub_z_kernel(tc, zT, wT, xm, wt, cs, offs, out):
                 )
 
         atoms = keep.tile([P, PACK * N], BF16, name="atoms", align_bytes=64)
-        w1_bf = keep.tile([P, D * PACK], BF16, name="w1_bf", align_bytes=64)
         w1_codes = keep.tile([P, D], U32, name="w1_codes", align_bytes=64)
         w1_scales = keep.tile([P, D], U8, name="w1_scales", align_bytes=64)
+        w_banks = []
+
+        def leave_bank(t, dst, copy_out):
+            copy_out(out=dst.bitcast(F32).rearrange("p (c u) -> p c u", u=2), in_=w_banks[t][:].rearrange("p u c -> p c u"))
+
+        def quantise_turned(first, count, src):
+            cols = slice(first * P, (first + count) * P)
+            nc.vector.quantize_mx(out=w1_codes[:, cols].bitcast(E4M3), scales=w1_scales[:, cols], in_=src)
+
+        last_two = keep.tile([P, 2 * P * PACK], BF16, name="w1_bf23", align_bytes=64)
         for t in range(PACK):
             nc.vector.tensor_copy(out=atoms[:, t * N : (t + 1) * N], in_=planes[t][:].indirect(offsets[:]))
             words = atoms[:, t * N : (t + 1) * N].bitcast(F32)
             bank = psum.tile([P, 2, P], F32, name="w_bank%d" % t, tag="turn", bufs=3)
             for u in range(2):
                 nc.tensor.transpose(bank[:, u, :], words[:, u : N // 2 : 2], ident[:])
-            dst = w1_bf[:, t * P * PACK : (t + 1) * P * PACK]
-            copy_out = nc.vector.tensor_copy if t == PACK - 1 else nc.scalar.copy
-            copy_out(out=dst.bitcast(F32).rearrange("p (c u) -> p c u", u=2), in_=bank[:].rearrange("p u c -> p c u"))
-            nc.vector.quantize_mx(
-                out=w1_codes[:, t * P : (t + 1) * P].bitcast(E4M3), scales=w1_scales[:, t * P : (t + 1) * P], in_=dst
-            )
+            w_banks.append(bank)
+            if t in (1, 2):
+                turned = keep.tile([P, P * PACK], BF16, name="w1_bf%d" % (t - 1), tag="plane%d" % t, align_bytes=64)
+                leave_bank(t - 1, turned[:], nc.scalar.copy)
+                quantise_turned(t - 1, 1, turned[:])
+            if t == 2:
+                leave_bank(2, last_two[:, : P * PACK], nc.scalar.copy)
+        leave_bank(3, last_two[:, P * PACK :], nc.vector.tensor_copy)
+        quantise_turned(2, 2, last_two[:])
 
         z_codes, z_scales = {}, {}
         diff = [keep.tile([P, D], F32, name="diff%d" % j) for j in range(TILES)]
@@ -114,17 +124,17 @@ def tile_attend_gdi_hub_z_kernel(tc, zT, wT, xm, wt, cs, offs, out):
             z_scales[j] = keep.tile([P, P], U8, name="z_scales%d" % j, align_bytes=64)
             nc.vector.quantize_mx(out=z_codes[j][:].bitcast(E4M3), scales=z_scales[j][:], in_=z_bf[:])
 
-        def weave_atoms(half, tag):
+        def weave_atoms(half, tag, copy):
             woven = keep.tile([P, 256 * PACK], BF16, name="w2_bf%d" % half, tag=tag, align_bytes=64)
             src = atoms[:].rearrange("p (t s) -> p t s", t=PACK)[:, :, half * 256 : (half + 1) * 256]
-            nc.vector.tensor_copy(
+            copy(
                 out=woven[:].rearrange("p (c i t) -> p c t i", i=4, t=PACK),
                 in_=src.rearrange("p t (c i) -> p c t i", i=4),
             )
             return woven
 
         def residual(j):
-            rec = psum.tile([P, D], F32, name="rec%d" % j, tag="rec", bufs=2)
+            rec = psum.tile([P, D], F32, name="rec%d" % j, tag="rec", bufs=3)
             nc.tensor.matmul_mx(
                 out=rec[:],
                 lhsT=z_codes[j][:].bitcast(E4M3),
@@ -171,7 +181,8 @@ def tile_attend_gdi_hub_z_kernel(tc, zT, wT, xm, wt, cs, offs, out):
             e_codes = keep.tile([P, P], U32, name="e_codes%d" % j, align_bytes=64)
             e_scales = keep.tile([P, P], U8, name="e_scales%d" % j, align_bytes=64)
             nc.vector.quantize_mx(out=e_codes[:].bitcast(E5M2), scales=e_scales[:], in_=e_bf[j][:])
-            acc = psum.tile([P, N], F32, name="acc%d" % j, tag="out", bufs=3)
+            tag, bufs = ("out", 2) if j < TILES - 2 else ("rec", 3)
+            acc = psum.tile([P, N], F32, name="acc%d" % j, tag=tag, bufs=bufs)
             nc.tensor.matmul_mx(
                 out=acc[:],
                 lhsT=e_codes[:].bitcast(E5M2),
@@ -198,18 +209,18 @@ def tile_attend_gdi_hub_z_kernel(tc, zT, wT, xm, wt, cs, offs, out):
 
         prepare_z(0)
         prepare_z(1)
-        woven = [weave_atoms(0, "w2_bf0")]
         residual(0)
         turn(0)
+        prepare_z(2)
         residual(1)
         turn(1)
-        woven.append(weave_atoms(1, "z_bf1"))
-        w2["codes"] = keep.tile([P, N], U32, name="w2_codes", tag="z_raw0", align_bytes=64)
-        w2["scales"] = keep.tile([P, N], U8, name="w2_scales", align_bytes=64)
-        prepare_z(2)
+        woven = [weave_atoms(0, "w2_bf0", nc.vector.tensor_copy), weave_atoms(1, "z_raw0", nc.scalar.copy)]
+        prepare_z(3)
         residual(2)
         turn(2)
-        prepare_z(3)
+        prepare_z(4)
+        w2["codes"] = keep.tile([P, N], U32, name="w2_codes", tag="z_bf0", align_bytes=64)
+        w2["scales"] = keep.tile([P, N], U8, name="w2_scales", align_bytes=64)
         for half in range(2):
             cols = slice(half * 256, (half + 1) * 256)
             nc.vector.quantize_mx(out=w2["codes"][:, cols].bitcast(E4M3), scales=w2["scales"][:, cols], in_=woven[half][:])
@@ -218,8 +229,8 @@ def tile_attend_gdi_hub_z_kernel(tc, zT, wT, xm, wt, cs, offs, out):
             if s + 3 < TILES:
                 residual(s + 3)
                 turn(s + 3)
-            if s + 4 < TILES:
-                prepare_z(s + 4)
+            if s + 5 < TILES:
+                prepare_z(s + 5)
             weigh(s)
             if s + 1 < TILES:
                 clip(s + 1)

@@ -117,8 +117,8 @@ def tile_attend_gdi_hub_z_kernel(tc, zT, wT, xm, wt, cs, offs, out):
         def prepare_z(j):
             z_bf = keep.tile([P, P * PACK], BF16, name="z_bf%d" % j, tag="z_bf%d" % j, align_bytes=64)
             nc.scalar.copy(
-                out=z_bf[:].rearrange("p (c i t) -> p c t i", i=2, t=PACK),
-                in_=z_raw[j].rearrange("p t (c i) -> p c t i", i=2),
+                out=z_bf[:].rearrange("p (r t) -> p r t", t=PACK),
+                in_=z_raw[j].rearrange("p t r -> p r t"),
             )
             z_codes[j] = keep.tile([P, P], U32, name="z_codes%d" % j, align_bytes=64)
             z_scales[j] = keep.tile([P, P], U8, name="z_scales%d" % j, align_bytes=64)
@@ -207,18 +207,18 @@ def tile_attend_gdi_hub_z_kernel(tc, zT, wT, xm, wt, cs, offs, out):
                     nc.vector.tensor_copy(out=result[:, cols], in_=acc[:, cols])
                     nc.sync.dma_start(out=rows[:, cols], in_=result[:, cols])
 
-        prepare_z(0)
-        prepare_z(1)
+        for j in range(3):
+            prepare_z(j)
         residual(0)
         turn(0)
-        prepare_z(2)
+        prepare_z(3)
         residual(1)
         turn(1)
-        woven = [weave_atoms(0, "w2_bf0", nc.vector.tensor_copy), weave_atoms(1, "z_raw0", nc.scalar.copy)]
-        prepare_z(3)
+        woven = [weave_atoms(0, "w2_bf0", nc.vector.tensor_copy), weave_atoms(1, "z_bf1", nc.vector.tensor_copy)]
+        prepare_z(4)
         residual(2)
         turn(2)
-        prepare_z(4)
+        prepare_z(5)
         w2["codes"] = keep.tile([P, N], U32, name="w2_codes", tag="z_bf0", align_bytes=64)
         w2["scales"] = keep.tile([P, N], U8, name="w2_scales", align_bytes=64)
         for half in range(2):
@@ -229,8 +229,8 @@ def tile_attend_gdi_hub_z_kernel(tc, zT, wT, xm, wt, cs, offs, out):
             if s + 3 < TILES:
                 residual(s + 3)
                 turn(s + 3)
-            if s + 5 < TILES:
-                prepare_z(s + 5)
+            if s + 6 < TILES:
+                prepare_z(s + 6)
             weigh(s)
             if s + 1 < TILES:
                 clip(s + 1)

from contextlib import ExitStack

import concourse.mybir as mybir
from concourse.masks import make_identity

N, T, D, R = 512, 2048, 512, 1024
FLOPS = 2 * 2 * R * N * D

F32 = mybir.dt.float32
BF16 = mybir.dt.bfloat16
U32 = mybir.dt.uint32
U16 = mybir.dt.uint16
U8 = mybir.dt.uint8
E4M3 = mybir.dt.float8_e4m3fn_x4
E5M2 = mybir.dt.float8_e5m2_x4
ALU = mybir.AluOpType
COPY = mybir.ActivationFunctionType.Copy

P = 128
PACK = 4
TILES = R // P
QR = 256
QUARTERS = R // QR


def tile_attend_gdi_hub_z_kernel(tc, zT, wT, xm, wt, cs, offs, out):
    nc = tc.nc
    with ExitStack() as ctx:
        keep = ctx.enter_context(tc.tile_pool(name="keep", bufs=1))
        psum = ctx.enter_context(tc.psum_pool(name="psum", bufs=1))

        offsets = keep.tile([P, N // 16], U16, name="offsets")
        nc.sync.dma_start(offsets[:], offs)
        wt_cols = keep.tile([P, 2, PACK], F32, name="wt_cols")
        nc.scalar.dma_start(out=wt_cols[:], in_=wt[0].rearrange("(h p j) o -> p h (j o)", h=2, j=PACK))
        cs_cols = keep.tile([P, PACK], F32, name="cs_cols")
        nc.scalar.dma_start(out=cs_cols[:], in_=cs[0:1, :].rearrange("o (p t) -> p (o t)", t=PACK))
        w_rows = wT.rearrange("(p t) n -> t p n", t=PACK)
        planes = []
        for t in range(PACK):
            plane = keep.tile([P, T], F32, name="plane%d" % t, tag="plane%d" % t, align_bytes=64)
            nc.sync.dma_start(out=plane[:], in_=w_rows[t])
            planes.append(plane)
        z_rows = zT[0].rearrange("(p j) r -> p j r", j=PACK)
        z_raw, x_raw = {}, {}

        def load_z(first, count):
            piece = keep.tile([P, PACK, count * P], F32, name="z_raw%d" % first, tag="z_raw%d" % first, align_bytes=64)
            nc.sync.dma_start(out=piece[:], in_=z_rows[:, :, first * P : (first + count) * P])
            for a in range(count):
                z_raw[first + a] = piece[:, :, a * P : (a + 1) * P]

        def load_x(first):
            piece = keep.tile([P, 2, D], F32, name="x_raw%d" % first)
            nc.sync.dma_start(
                out=piece[:], in_=xm[0, first * P : (first + 2) * P, :].rearrange("(a m) d -> m a d", a=2)
            )
            for a in range(2):
                x_raw[first + a] = piece[:, a, :]

        for half in range(2):
            load_z(4 * half, 2)
            load_z(4 * half + 2, 2)
            load_x(4 * half)
            load_x(4 * half + 2)

        ident = keep.tile([P, P], F32, name="ident")
        make_identity(nc, ident[:])

        factor = keep.tile([P, PACK * R], F32, name="factor")
        for h in range(2):
            bank = psum.tile([P, PACK, P], F32, name="wt_bank%d" % h, tag="out", bufs=2)
            for j in range(PACK):
                nc.tensor.transpose(bank[:, j, :], wt_cols[:, h, j : j + 1].to_broadcast([P, P]), ident[:])
            for t in range(PACK):
                nc.scalar.activation(
                    out=factor[:, t * R + h * 512 : t * R + (h + 1) * 512].rearrange("p (m j) -> p m j", j=PACK),
                    in_=bank[:].rearrange("p j m -> p m j"),
                    func=COPY,
                    scale=cs_cols[:, t : t + 1],
                )

        atoms = keep.tile([P, PACK * N], BF16, name="atoms", align_bytes=64)
        w1_codes = keep.tile([P, D], U32, name="w1_codes", align_bytes=64)
        w1_scales = keep.tile([P, D], U8, name="w1_scales", align_bytes=64)
        w_banks = []

        def leave_bank(t, dst, copy_out):
            copy_out(out=dst.bitcast(F32).rearrange("p (c u) -> p c u", u=2), in_=w_banks[t][:].rearrange("p u c -> p c u"))

        def quantise_turned(first, count, src):
            cols = slice(first * P, (first + count) * P)
            nc.vector.quantize_mx(out=w1_codes[:, cols].bitcast(E4M3), scales=w1_scales[:, cols], in_=src)

        last_two = keep.tile([P, 2 * P * PACK], BF16, name="w1_bf23", align_bytes=64)
        for t in range(PACK):
            nc.vector.tensor_copy(out=atoms[:, t * N : (t + 1) * N], in_=planes[t][:].indirect(offsets[:]))
            words = atoms[:, t * N : (t + 1) * N].bitcast(F32)
            bank = psum.tile([P, 2, P], F32, name="w_bank%d" % t, tag="turn", bufs=3)
            for u in range(2):
                nc.tensor.transpose(bank[:, u, :], words[:, u : N // 2 : 2], ident[:])
            w_banks.append(bank)
            if t in (1, 2):
                turned = keep.tile([P, P * PACK], BF16, name="w1_bf%d" % (t - 1), tag="plane%d" % t, align_bytes=64)
                leave_bank(t - 1, turned[:], nc.scalar.copy)
                quantise_turned(t - 1, 1, turned[:])
            if t == 2:
                leave_bank(2, last_two[:, : P * PACK], nc.scalar.copy)
        leave_bank(3, last_two[:, P * PACK :], nc.vector.tensor_copy)
        quantise_turned(2, 2, last_two[:])

        z_codes, z_scales = {}, {}
        diff = [keep.tile([P, D], F32, name="diff%d" % j) for j in range(TILES)]
        scaled, clipped, w2, accs = {}, {}, {}, {}
        e_bf = [keep.tile([P, P * PACK], BF16, name="e_bf%d" % j, align_bytes=64) for j in range(TILES)]

        def prepare_z(j):
            z_bf = keep.tile([P, P * PACK], BF16, name="z_bf%d" % j, tag="z_bf%d" % j, align_bytes=64)
            nc.scalar.copy(
                out=z_bf[:].rearrange("p (r t) -> p r t", t=PACK),
                in_=z_raw[j].rearrange("p t r -> p r t"),
            )
            z_codes[j] = keep.tile([P, P], U32, name="z_codes%d" % j, align_bytes=64)
            z_scales[j] = keep.tile([P, P], U8, name="z_scales%d" % j, align_bytes=64)
            nc.vector.quantize_mx(out=z_codes[j][:].bitcast(E4M3), scales=z_scales[j][:], in_=z_bf[:])

        def weave_atoms(half, tag, copy):
            woven = keep.tile([P, 256 * PACK], BF16, name="w2_bf%d" % half, tag=tag, align_bytes=64)
            src = atoms[:].rearrange("p (t s) -> p t s", t=PACK)[:, :, half * 256 : (half + 1) * 256]
            copy(
                out=woven[:].rearrange("p (c i t) -> p c t i", i=4, t=PACK),
                in_=src.rearrange("p t (c i) -> p c t i", i=4),
            )
            return woven

        def residual(j):
            rec = psum.tile([P, D], F32, name="rec%d" % j, tag="rec", bufs=3)
            nc.tensor.matmul_mx(
                out=rec[:],
                lhsT=z_codes[j][:].bitcast(E4M3),
                lhsT_scale=z_scales[j][:],
                rhs=w1_codes[:].bitcast(E4M3),
                rhs_scale=w1_scales[:],
                start=True,
                stop=True,
            )
            nc.vector.tensor_tensor(
                out=diff[j][:].rearrange("m (u p e) -> m u p e", u=2, e=2),
                in0=rec[:].rearrange("m (u e p) -> m u p e", u=2, e=2),
                in1=x_raw[j].rearrange("m (p u e) -> m u p e", u=2, e=2),
                op=ALU.subtract,
            )

        def turn(j):
            scaled[j] = keep.tile([P, PACK * P], F32, name="scaled%d" % j)
            bank = psum.tile([P, PACK, P], F32, name="d_bank%d" % j, tag="turn", bufs=3)
            for t in range(PACK):
                u, e = divmod(t, 2)
                nc.tensor.transpose(bank[:, t, :], diff[j][:, u * 256 + e : (u + 1) * 256 : 2], ident[:])
            for t in range(PACK):
                nc.scalar.activation(
                    out=scaled[j][:, t * P : (t + 1) * P], in_=bank[:, t, :], func=COPY, scale=cs_cols[:, t : t + 1]
                )

        def clip(j):
            clipped[j] = keep.tile([P, PACK * P], F32, name="clipped%d" % j)
            nc.vector.tensor_scalar(
                out=clipped[j][:], in0=scaled[j][:], scalar1=-1.0, scalar2=1.0, op0=ALU.max, op1=ALU.min
            )

        def weigh(j):
            f_view = factor[:].rearrange("p (t r) -> p t r", t=PACK)[:, :, j * P : (j + 1) * P]
            nc.vector.tensor_tensor(
                out=e_bf[j][:].rearrange("p (c i t) -> p c t i", i=2, t=PACK),
                in0=clipped[j][:].rearrange("p (t c i) -> p c t i", t=PACK, i=2),
                in1=f_view.rearrange("p t (c i) -> p c t i", i=2),
                op=ALU.mult,
            )

        def gradient(j):
            e_codes = keep.tile([P, P], U32, name="e_codes%d" % j, align_bytes=64)
            e_scales = keep.tile([P, P], U8, name="e_scales%d" % j, align_bytes=64)
            nc.vector.quantize_mx(out=e_codes[:].bitcast(E5M2), scales=e_scales[:], in_=e_bf[j][:])
            tag, bufs = ("out", 2) if j < TILES - 2 else ("rec", 3)
            acc = psum.tile([P, N], F32, name="acc%d" % j, tag=tag, bufs=bufs)
            nc.tensor.matmul_mx(
                out=acc[:],
                lhsT=e_codes[:].bitcast(E5M2),
                lhsT_scale=e_scales[:],
                rhs=w2["codes"][:].bitcast(E4M3),
                rhs_scale=w2["scales"][:],
                start=True,
                stop=True,
            )
            accs[j] = acc

        def store(j):
            acc = accs[j]
            result = keep.tile([P, N], F32, name="result%d" % j)
            rows = out[0, j * P : (j + 1) * P, :]
            if j < TILES - 1:
                nc.scalar.copy(out=result[:], in_=acc[:])
                nc.sync.dma_start(out=rows, in_=result[:])
            else:
                for half in range(2):
                    cols = slice(half * 256, (half + 1) * 256)
                    nc.vector.tensor_copy(out=result[:, cols], in_=acc[:, cols])
                    nc.sync.dma_start(out=rows[:, cols], in_=result[:, cols])

        for j in range(3):
            prepare_z(j)
        residual(0)
        turn(0)
        prepare_z(3)
        residual(1)
        turn(1)
        woven = [weave_atoms(0, "w2_bf0", nc.vector.tensor_copy), weave_atoms(1, "z_bf1", nc.vector.tensor_copy)]
        prepare_z(4)
        residual(2)
        turn(2)
        prepare_z(5)
        w2["codes"] = keep.tile([P, N], U32, name="w2_codes", tag="z_bf0", align_bytes=64)
        w2["scales"] = keep.tile([P, N], U8, name="w2_scales", align_bytes=64)
        for half in range(2):
            cols = slice(half * 256, (half + 1) * 256)
            nc.vector.quantize_mx(out=w2["codes"][:, cols].bitcast(E4M3), scales=w2["scales"][:, cols], in_=woven[half][:])
        clip(0)
        for s in range(TILES):
            if s + 3 < TILES:
                residual(s + 3)
                turn(s + 3)
            if s + 6 < TILES:
                prepare_z(s + 6)
            weigh(s)
            if s + 1 < TILES:
                clip(s + 1)
            gradient(s)
            if s >= 1:
                store(s - 1)
        store(TILES - 1)
